import numpy as np, ml_dtypes
CORES = [10,34,74,98]
N = 4
BF = ml_dtypes.bfloat16
def gentries(a):
    return np.ascontiguousarray(a.reshape(8, 16, -1).transpose(0, 2, 1)).reshape(8, -1)
def gtable(e):
    e = np.asarray(e); return np.ascontiguousarray(e.reshape(8, -1, 16).transpose(0, 2, 1)).reshape(128, -1).astype(np.int32)
M, B, H, ST = 224, 16, 4, 4
W = M * B
def parts(rng):
    c = np.minimum((W * np.exp2(-5 * rng.random((N, 8, 1, W))) * rng.random((N, 8, 16, W))).astype(np.int64), W - 1)
    a = np.exp2(5 * rng.random((N, 8, 16, 1))); q = rng.choice(np.array([1, 1, 1, 16, 256]), (N, 8, 16, 1))
    l = np.minimum((W * rng.random((N, 8, 16, W)) ** a).astype(np.int64), W - 1) & -q
    gap = np.minimum((W * (0.1 + 0.8 * rng.random((N, 8, 1, M))) * (0.5 + rng.random((N, 8, 16, M)))).astype(np.int64), W - 1)
    return c, l, gap, rng.integers(0, B, (N, 8, M))
def pack(c, l, gap, cur):
    return {"ck": np.ascontiguousarray(c.reshape(N, 128, W)).astype(np.int32), "la": np.ascontiguousarray(l.reshape(N, 128, W)).astype(np.int32),
            "gap": np.ascontiguousarray(gap.reshape(N, 128, M)).astype(np.int32), "cu": np.stack([gtable(a) for a in cur])}
def setup_inputs(rng):
    return pack(*parts(rng))
def setup_inputs_ties(rng):
    c, l, gap, cur = parts(rng); c = c & -64; gap = gap & -64; l = l & -64
    kind = rng.integers(0, 4, (N, 8, 16, 1)); kind[:, :, :4, 0] = np.arange(4)
    few = np.take_along_axis(rng.integers(0, W, (N, 8, 16, 4)), rng.integers(0, kind + 1, (N, 8, 16, W)), 3)
    l[:, ::2] = few[:, ::2]
    gap = np.where((rng.random((N, 8, 1, M)) < 0.25) & (rng.random((N, 8, 16, M)) < 0.2), 0, gap)
    return pack(c, l, gap, cur)
def setup_inputs_alike(rng):
    c, l, gap, cur = parts(rng)
    c[:, ::2] = np.maximum(c[:, ::2, :1], 16); c[:, ::2, :, 0] = rng.integers(0, 16, (N, 4, 16))
    c[:, 1::2] = rng.choice(np.array([3, W // 3, W // 2, W - 1]), (N, 4, 16, W))
    cur[:, :, 0] = 0; gap[:, :, :, 0] = 0
    return pack(c, l, gap, cur)
def setup_inputs_ends(rng):
    c, l, gap, cur = parts(rng)
    c[:, 0:4] = rng.choice(np.array([0, 1, W - 2, W - 1]), (N, 4, 16, W))
    l[:, 2:6] = rng.choice(np.array([0, 1, W - 2, W - 1]), (N, 4, 16, W))
    gap[:, 1:7] = rng.choice(np.array([0, 1, W - 1]), (N, 6, 16, M))
    cur = rng.choice(np.array([0, B - 1]), (N, 8, M))
    return pack(c, l, gap, cur)
def setup_inputs_count(rng):
    c, l, gap, cur = parts(rng); c = np.maximum(c, 1)
    n = rng.choice(np.array([0, H - 1, H, H + 1, 16]), (N, 8, 1, M)); g = rng.permutation(8)
    n[:, g[0]] = 16; n[:, g[1]] = 0; n[:, g[2], 0, :5] = np.array([0, H - 1, H, H + 1, 16])
    cur[:, g[0], :B] = np.arange(B)
    n[0::2, g[3]] = 16; n[1::2, g[3]] = 0
    n[:, g[4]] = 16; l[:, g[4]] = l[:, g[4], :, :1].copy(); c[:, g[4], :, 0] = 0
    cur[:, g[4], 0] = 1; cur[:, g[4], 1:9] = (2 * np.arange(N)[:, None] + np.arange(8)) & (B - 1)
    gap = np.where(np.argsort(rng.random((N, 8, 16, M)), axis=2) < n, 0, W - 1)
    return pack(c, l, gap, cur)
def setup_inputs_spread(rng):
    c, l, gap, cur = parts(rng); e = np.log2(W)
    c = np.minimum((np.exp2(e * rng.random((N, 8, 1, W))) * rng.random((N, 8, 16, W))).astype(np.int64), W - 1)
    l = np.minimum(np.exp2(e * rng.random((N, 8, 16, W)) ** (2 * rng.random((N, 8, 16, 1)))).astype(np.int64), W - 1)
    gap = np.minimum((np.exp2(e * (1 - rng.random((N, 8, 1, M)) ** 3)) * rng.random((N, 8, 16, M))).astype(np.int64), W - 1)
    return pack(c, l, gap, cur)
def check_inputs(d):
    bad = []
    for k, hi in (("ck", W - 1), ("la", W - 1), ("gap", W - 1), ("cu", B - 1)):
        if np.min(d[k]) < 0 or np.max(d[k]) > hi: bad.append("range of " + k)
    return bad
def columns(t, x):
    return np.take_along_axis(t, np.swapaxes(x, 2, 3).reshape(N, 8, 1, 16 * M), 3).reshape(N, 8, 16, M, 16)
def reference(ck, la, gap, cu):
    C = ck.astype(np.int64).reshape(N, 8, 16, W); L = la.astype(np.int64).reshape(N, 8, 16, W); G = gap.astype(np.int64).reshape(N, 8, 16, M)
    cur = np.stack([gentries(a) for a in cu]).astype(np.int64); first = B * np.arange(M)
    I = np.take_along_axis(C, (first + cur)[:, :, None, :], 3); T = I + G
    for step in range(ST):
        A = columns(L, I); top = np.max(A, axis=4, keepdims=True)
        s = np.max(np.where(A < top, A, 0), axis=4)
        I = np.maximum(I, np.max(columns(C, s), axis=4))
        out = np.add.reduce((I >= T).astype(np.int64), axis=2) >= H
        hit = (np.arange(B) == cur[..., None]) & out[..., None]
        C = np.where(hit[:, :, None], I[..., None], C.reshape(N, 8, 16, M, B)).reshape(N, 8, 16, W)
        cur = np.where(out, (cur + 1) & (B - 1), cur)
        new = np.take_along_axis(C, (first + cur)[:, :, None, :], 3)
        T = np.where(out[:, :, None], new + G, T); I = np.where(out[:, :, None], new, I)
        I, T, G, cur = np.roll(I, 1, axis=0), np.roll(T, 1, axis=0), np.roll(G, 1, axis=0), np.roll(cur, 1, axis=0)
    return {"yi": I.reshape(N, 128, M).astype(np.float32), "yc": np.stack([gtable(a) for a in cur]).astype(np.float32)}

@@ -1,0 +1,436 @@
+import math
+from concourse.bass import DstId, RemoteDMATransfer
+from concourse.mybir import dt, AluOpType, AxisListType, ActivationFunctionType
+
+W = 3584
+M = 224
+ST = 4
+NQ = 14
+SIZES = [64, 64, 48, 48]
+CHUNKS = []
+_a = 0
+for _n in SIZES:
+    CHUNKS.append((_a, _a + _n))
+    _a += _n
+NC = len(CHUNKS)
+PIECES = 4
+PW = W // PIECES
+KE = 512.0
+KV = float(2 ** 60)
+SC = 32.0 / math.log(2.0)
+B0 = -100.0 * math.log(2.0)
+UP = 2.0 ** 50
+OFF = 1600.0
+EPS = 2.0 ** -62
+CW, CT, CR, CE = 32, 48, 272, 496
+
+SCRATCH = {}
+
+
+def _declare():
+    def sb(names, n, t):
+        for x in names.split():
+            SCRATCH[x] = ("sbuf", [128, n], t)
+
+    sb("ck32 la32", W, "int32")
+    sb("cf lf", W, "float32")
+    sb("Cc", W + M, "bfloat16")
+    sb("Lc", W, "bfloat16")
+    sb("cu32 il32 nx nxa rl32 pt pa q16 cl c16", NQ, "int32")
+    sb("gap32 yint", M, "int32")
+    sb("gapf gc0 gc1 gc2 lnI lnS yout", M, "float32")
+    sb("il rl", NQ, "uint16")
+    sb("Iu su", M, "uint16")
+    sb("Inew Rld R s1 s2", M, "bfloat16")
+    sb("AA m3 pm", 42, "float32")
+    sb("c15", NQ, "float32")
+    sb("lst", 28, "uint16")
+    sb("mask", 1024, "bfloat16")
+    sb("fK fN idK idN fP fQ bP1 bP bQ1 bQ hP hQ", 128, "bfloat16")
+    sb("fE e1 e2 e3", 144, "bfloat16")
+    sb("one", 64, "bfloat16")
+    for t in range(ST + 1):
+        sb("Ic%d" % t, M, "bfloat16")
+        sb("TW%d" % t, CE, "float32")
+    for t in range(ST):
+        sb("MS%d" % t, CR, "float32")
+        sb("IP%d" % t, M, "bfloat16")
+    for j, n in enumerate(SIZES):
+        sb("x%d y%d P%d u%d z%d q%d" % (j, j, j, j, j, j), n * 16, "bfloat16")
+    for k in range(8):
+        SCRATCH["ps%d" % k] = ("psum", [128, 512], "float32")
+
+
+_declare()
+BANKS = []
+_b = 0
+for _n in SIZES:
+    _k = -(-_n * 16 // 512)
+    BANKS.append(list(range(_b, _b + _k)))
+    _b += _k
+CB = min(_b, 7)
+
+SEMAPHORES = ["vec", "act", "ten", "gps", "loc", "gap"]
+for _t in range(ST):
+    SEMAPHORES += ["a%d_%d" % (_t, _j) for _j in range(NC)] + ["b%d" % _t]
+SEMAPHORES += ["ld%d" % _k for _k in range(2 * PIECES + 2)] + ["st%d" % _k for _k in range(NC + 1)]
+
+COST = {"cy": 0.83e-3 * 1.25, "gather": 1.56, "scatter": 3.8, "fix": 0.03, "gfix": 0.07, "lat": 0.08, "net": 2.2, "send": 0.9,
+        "mm": 0.046 * 1.25, "ld0": 2.0, "ld": 2.3, "st": 2.0}
+
+
+def dur(ck, c):
+    k, n = ck
+    if k == "v":
+        return c["fix"] + max(64, n) * c["cy"]
+    if k == "s":
+        return c["gfix"] + max(32, n) * c["cy"]
+    if k == "gather":
+        return c["gfix"] + n * c["gather"] * c["cy"]
+    if k == "scatter":
+        return c["gfix"] + n * c["scatter"] * c["cy"]
+    if k == "mm":
+        return n * c["mm"]
+    if k == "sel":
+        return 0.2 + 2 * n * c["cy"]
+    if k == "ld":
+        return c["ld0"] + n * c["ld"]
+    if k == "us":
+        return n
+    return n * c[k]
+
+
+def plan(ops, c=COST, jit=None):
+    n = len(ops)
+    cost = [dur(o["ck"], c) for o in ops]
+    lat = c["lat"]
+    succ = [[] for _ in range(n)]
+    for i, o in enumerate(ops):
+        for d in o["deps"]:
+            succ[d].append(i)
+    prio = [0.0] * n
+    for i in range(n - 1, -1, -1):
+        best = 0.0
+        for k in succ[i]:
+            best = max(best, prio[k] + lat)
+        prio[i] = cost[i] + best
+    if jit:
+        prio = [p + j for p, j in zip(prio, jit)]
+    left = [len(o["deps"]) for o in ops]
+    est = [0.0] * n
+    ready = [i for i in range(n) if left[i] == 0]
+    fin = [0.0] * n
+    free = {}
+    order = []
+    beg = [0.0] * n
+    while ready:
+        pick, key = None, None
+        for i in ready:
+            q = ops[i]["q"]
+            s = est[i] if q == "X" else max(est[i], free.get(q, 0.0))
+            if key is None or (s, -prio[i]) < key:
+                pick, key = i, (s, -prio[i])
+        q = ops[pick]["q"]
+        ready.remove(pick)
+        order.append(pick)
+        beg[pick] = key[0]
+        fin[pick] = key[0] + cost[pick]
+        if q != "X":
+            free[q] = fin[pick]
+        for k in succ[pick]:
+            left[k] -= 1
+            est[k] = max(est[k], fin[pick] + lat)
+            if left[k] == 0:
+                ready.append(k)
+    return order, beg, fin
+
+
+def build(g, T, topo, core, rank):
+    A, F = AluOpType, ActivationFunctionType
+    ops = []
+    hist = {}
+
+    def op(q, ck, fn, reads=(), writes=(), sem=None, deps=(), kind="c", name=""):
+        i = len(ops)
+        dd = set(deps)
+        for lst, wr in ((reads, False), (writes, True)):
+            for (b, lo, hi) in lst:
+                for (l2, h2, k, w2) in hist.get(b, ()):
+                    if k != i and l2 < hi and lo < h2 and (wr or w2):
+                        dd.add(k)
+        for (b, lo, hi) in writes:
+            h = hist.get(b, [])
+            hist[b] = [e for e in h if not (lo <= e[0] and e[1] <= hi)] + [(lo, hi, i, True)]
+        for (b, lo, hi) in reads:
+            hist.setdefault(b, []).append((lo, hi, i, False))
+        ops.append({"q": q, "ck": ck, "fn": fn, "deps": dd, "sem": sem, "kind": kind, "name": name})
+        return i
+
+    def V(n, fn, reads, writes, name=""):
+        return op("V", ("v", n), fn, reads, writes, name=name)
+
+    def S(n, fn, reads, writes, name="", deps=()):
+        return op("S", ("s", n), fn, reads, writes, name=name, deps=deps)
+
+    def SG(n, fn, reads, writes, name=""):
+        return op("S", ("gather", n), fn, reads, writes, name=name)
+
+    def full(b):
+        return (b, 0, 1 << 20)
+
+    v, sc, te, sy = g.vector, g.scalar, g.tensor, g.sync
+
+    def fill(b, n, c):
+        V(n, lambda: v.memset(T[b][:], c), [], [full(b)], "fill")
+
+    fill("fK", 64, KE)
+    fill("fN", 64, -KE)
+    fill("fP", 64, KV)
+    fill("fQ", 64, -KV)
+    fill("fE", 64, 1.0)
+    fill("hP", 64, -3.5 * KV)
+    fill("hQ", 64, 3.5 * KV)
+    fill("one", 64, 1.0)
+    fill("mask", 512, 1.0)
+    V(64, lambda: v.memset(T.mask[:, 0::16], 0.0), [], [full("mask")], "mask")
+    V(64, lambda: v.memset(T.AA[:, 14:28], float(M)), [], [("AA", 14, 28)], "AA")
+    for t in range(ST):
+        V(64, lambda t=t: v.memset(T["MS%d" % t][:, CW:CT], 0.0), [], [("MS%d" % t, CW, CT)], "MSpad")
+
+    def sel(out, src, n, pattern, cmp, base, cm):
+        op("G", ("sel", n), lambda: g.affine_select(T[out][:], T[src][:], pattern, cmp, 0.0, base, cm), [full(src)], [full(out)], name="sel")
+
+    op("G", ("us", 0.2), lambda: g.iota(T.pt[:], [[0, NQ]], 0, 1), [], [full("pt")], name="iota")
+    op("G", ("us", 0.2), lambda: g.iota(T.q16[:], [[16, NQ]], 0, 0), [], [full("q16")], name="iota")
+    sel("idK", "fK", 128, [[-1, 128]], A.is_equal, 0, 1)
+    sel("idN", "fN", 128, [[-1, 128]], A.is_equal, 0, 1)
+    sel("bP1", "fP", 128, [[-16, 8], [0, 16]], A.is_ge, 0, 1)
+    sel("bP", "bP1", 128, [[16, 8], [0, 16]], A.is_ge, 15, -1)
+    sel("bQ1", "fQ", 128, [[-16, 8], [0, 16]], A.is_ge, 0, 1)
+    sel("bQ", "bQ1", 128, [[16, 8], [0, 16]], A.is_ge, 15, -1)
+    sel("e1", "fE", 144, [[0, 9], [1, 16]], A.is_equal, -15, 0)
+    sel("e2", "e1", 144, [[-16, 9], [0, 16]], A.is_ge, 0, 1)
+    sel("e3", "e2", 144, [[16, 9], [0, 16]], A.is_ge, 15, -1)
+
+    V(NQ, lambda: v.tensor_scalar(T.pa[:], T.pt[:], 15, None, A.bitwise_and), [full("pt")], [full("pa")])
+    V(NQ, lambda: v.tensor_tensor(T.cl[:], T.pa[:], T.q16[:], A.add), [full("pa"), full("q16")], [full("cl")])
+    V(NQ, lambda: v.tensor_scalar(T.c16[:], T.cl[:], 16.0, None, A.mult), [full("cl")], [full("c16")])
+    V(NQ, lambda: v.tensor_scalar(T.c15[:], T.cl[:], 15.0, float(-W), A.mult, A.add), [full("cl")], [full("c15")])
+    for t in range(ST - 1):
+        b = "TW%d" % t
+        V(NQ, lambda b=b: v.tensor_scalar(T[b][:, 4:18], T.cl[:], float(W), None, A.add), [full("cl")], [(b, 4, 18)])
+        V(NQ, lambda b=b: v.tensor_scalar(T[b][:, 18:32], T.cl[:], 1.0, None, A.mult), [full("cl")], [(b, 18, 32)])
+
+    dq = {"sync": ("Y", sy), "act": ("S", sc)}
+
+    def load(which, k, out, in_, b, lo, hi, n):
+        q, e = dq[which]
+        i = op(q, ("us", 0.06), lambda: e.dma_start(out, in_), [], [], sem="ld%d" % k, kind="dma", name="ld")
+        op("X", ("ld", n), None, [], [(b, lo, hi)], sem=("ld%d" % k, 16), kind="arr", deps=[i], name="land")
+
+    load("sync", 2 * PIECES, T.cu32[:], T.cu[:], "cu32", 0, NQ, 0)
+    k = 0
+    for b, src in (("ck32", T.ck), ("la32", T.la)):
+        for p in range(PIECES):
+            lo, hi = p * PW, (p + 1) * PW
+            load("sync" if p % 2 == 0 else "act", k, T[b][:, lo:hi], src[:, lo:hi], b, lo, hi, k + 1)
+            k += 1
+        if b == "ck32":
+            load("act", 2 * PIECES + 1, T.gap32[:], T.gap[:], "gap32", 0, M, k)
+
+    V(NQ, lambda: v.tensor_copy(T.TW0[:, CW:CW + NQ], T.cu32[:]), [full("cu32")], [("TW0", CW, CW + NQ)])
+    V(NQ, lambda: v.tensor_tensor(T.il32[:], T.cu32[:], T.c16[:], A.add), [full("cu32"), full("c16")], [full("il32")])
+    V(NQ, lambda: v.tensor_copy(T.il[:], T.il32[:]), [full("il32")], [full("il")])
+    op("V", ("gather", M), lambda: v.tensor_copy(T.Iu[:], T.ck32[:].indirect(T.il[:])), [full("ck32"), full("il")], [full("Iu")], name="Iu0")
+    lastexp = []
+    for b, f, o in (("ck32", "cf", "Cc"), ("la32", "lf", "Lc")):
+        for p in range(PIECES):
+            lo, hi = p * PW, (p + 1) * PW
+            V(PW, lambda b=b, f=f, lo=lo, hi=hi: v.tensor_copy(T[f][:, lo:hi], T[b][:, lo:hi]), [(b, lo, hi)], [(f, lo, hi)], "conv")
+            lastexp.append(S(PW, lambda f=f, o=o, lo=lo, hi=hi: sc.activation(T[o][:, lo:hi], T[f][:, lo:hi], F.Exp, bias=B0, scale=1.0 / SC),
+                             [(f, lo, hi)], [(o, lo, hi)], name="exp"))
+    V(M, lambda: v.tensor_scalar(T.gapf[:], T.gap32[:], 0.5, None, A.subtract), [full("gap32")], [full("gapf")])
+    lastexp.append(S(M, lambda: sc.activation(T.gc0[:], T.gapf[:], F.Exp, scale=1.0 / SC), [full("gapf")], [full("gc0")], name="expg"))
+
+    nloc = [0]
+    cores = list(T.cores)
+    nxt = cores[(rank + 1) % len(cores)]
+
+    def send_gap():
+        dst = [cores[(rank + d) % len(cores)] for d in (1, 2)]
+        eng = [e for e in topo.engines(core, dst[0]) if e in topo.engines(core, dst[1])]
+        m = 0
+        for e in eng:
+            m |= 1 << e
+        ids = []
+        for d in dst:
+            a = topo.addr(d)
+            ids.append(DstId(rid=a[0], pnc=a[1]))
+        nloc[0] += len(eng)
+        g.remote_dma_fused([RemoteDMATransfer(dst_ids=ids, dma_engine_mask=m, remote_sem=T.sem.gap, srcs=[T.gc0[:]], dsts=[T.gc1[:], T.gc2[:]])], local_sem=T.sem.loc)
+
+    i = op("G", ("send", 1), send_gap, [full("gc0")], [], kind="send", name="gap")
+    ne = len(topo.engines(core, nxt))
+    op("X", ("us", 5.0), None, [], [full("gc1"), full("gc2")], sem=("gap", 2 * ne), kind="arr", deps=[i], name="agap")
+
+    def send(out, in_, sem):
+        a = topo.addr(nxt)
+        nloc[0] += ne
+        g.remote_dma(out, in_, T.sem[sem], T.sem.loc, a[1], a[0], topo.mask(core, nxt))
+
+    SG(M, lambda: sc.activation(T.Ic0[:], T.Cc[:, 0:W].indirect(T.il[:]), F.Copy), [("Cc", 0, W), full("il")], [full("Ic0")], name="Ic0")
+    V(2 * M, lambda: v.tensor_tensor(T.TW0[:, CT:CR], T.Ic0[:], T.gc0[:], A.mult), [full("Ic0"), full("gc0")], [("TW0", CT, CR)], "Tc0")
+
+    def step(t):
+        last = t == ST - 1
+        IC, TW, MS, IP = "Ic%d" % t, "TW%d" % t, "MS%d" % t, "IP%d" % t
+        Icb, TWb, MSb, IPb = T[IC], T[TW], T[MS], T[IP]
+        for j, (a, e) in enumerate(CHUNKS):
+            n = e - a
+            xb, yb, Pb, ub = T["x%d" % j], T["y%d" % j], T["P%d" % j], T["u%d" % j]
+            X, Y, P, U = "x%d" % j, "y%d" % j, "P%d" % j, "u%d" % j
+            if t > 0:
+                S(n, lambda a=a, e=e: sc.activation(T.lnI[:, a:e], Icb[:, a:e], F.Ln, scale=UP), [(IC, a, e)], [("lnI", a, e)], name="lnI%d" % j)
+                V(n, lambda a=a, e=e: v.tensor_scalar(T.Iu[:, a:e], T.lnI[:, a:e], SC, OFF + 0.25, A.mult, A.add), [("lnI", a, e)], [("Iu", a, e)], "decI%d" % j)
+            SG(16 * n, lambda a=a, e=e, xb=xb: sc.activation(xb[:], T.Lc[:].indirect(T.Iu[:, a:e]), F.Copy), [full("Lc"), ("Iu", a, e)], [full(X)], name="G1_%d" % j)
+            V(8 * n, lambda n=n, xb=xb, Pb=Pb: v.tensor_tensor_scan(Pb[:], T.mask[:, 0:16 * n], xb[:], 0.0, A.mult, A.max), [full("mask"), full(X)], [full(P)], "scan1_%d" % j)
+            bk = BANKS[j]
+            per = 16 // len(bk)
+
+            def diff(n=n, xb=xb, Pb=Pb, bk=bk, per=per):
+                for h, b in enumerate(bk):
+                    te.matmul(T["ps%d" % b][:, 0:per * n], T.idN[:], xb[:, h::len(bk)], True, False)
+                    for i in range(per):
+                        r = te.matmul(T["ps%d" % b][:, i:per * n:per], T.idK[:], Pb[:, 15::16], False, i == per - 1)
+                return r
+
+            op("P", ("mm", 16 + 16 * n / 64), diff, [full("idK"), full("idN"), full(P), full(X)], [full("ps%d" % b) for b in bk], name="diff%d" % j)
+            for h, b in enumerate(bk):
+                V(per * n, lambda n=n, xb=xb, yb=yb, h=h, b=b, per=per, bk=bk: v.tensor_tensor(yb[:, h::len(bk)], xb[:, h::len(bk)], T["ps%d" % b][:, 0:per * n], A.min),
+                  [full(X), full("ps%d" % b)], [(Y, h, h + 1)], "min%d_%d" % (j, h))
+            V(8 * n, lambda n=n, yb=yb, ub=ub: v.tensor_tensor_scan(ub[:], T.mask[:, 0:16 * n], yb[:], 0.0, A.mult, A.max), [full("mask"), full(Y)], [full(U)], "scan2_%d" % j)
+            S(n, lambda a=a, e=e, ub=ub: sc.activation(T.lnS[:, a:e], ub[:, 15::16], F.Ln, bias=EPS, scale=UP), [full(U)], [("lnS", a, e)],
+              deps=lastexp if t == 0 else (), name="lnS%d" % j)
+            V(n, lambda a=a, e=e: v.tensor_scalar(T.su[:, a:e], T.lnS[:, a:e], SC, OFF + 0.25, A.mult, A.add), [("lnS", a, e)], [("su", a, e)], "decS%d" % j)
+        V(NQ, lambda: v.tensor_scalar(T.nxa[:], TWb[:, CW:CW + NQ], 1.0, None, A.add), [(TW, CW, CW + NQ)], [full("nxa")])
+        V(NQ, lambda: v.tensor_scalar(T.nx[:], T.nxa[:], 15, None, A.bitwise_and), [full("nxa")], [full("nx")])
+        V(NQ, lambda: v.tensor_tensor(T.rl32[:], T.nx[:], T.c16[:], A.add), [full("nx"), full("c16")], [full("rl32")])
+        V(NQ, lambda: v.tensor_copy(T.rl[:], T.rl32[:]), [full("rl32")], [full("rl")])
+        V(NQ, lambda: v.tensor_tensor(T.AA[:, 28:42], T.nx[:], TWb[:, CW:CW + NQ], A.subtract), [full("nx"), (TW, CW, CW + NQ)], [("AA", 28, 42)])
+        if not last:
+            V(NQ, lambda: v.tensor_tensor(T.AA[:, 0:14], T.c15[:], TWb[:, CW:CW + NQ], A.add), [full("c15"), (TW, CW, CW + NQ)], [("AA", 0, 14)])
+        SG(M, lambda: sc.activation(T.Rld[:], T.Cc[:, 0:W].indirect(T.rl[:]), F.Copy), [("Cc", 0, W), full("rl")], [full("Rld")], name="Rld")
+        if not last:
+            gb = "gc%d" % t
+            V(2 * M, lambda: v.tensor_tensor(TWb[:, CR:CE], T.Rld[:], T[gb][:], A.mult), [full("Rld"), full(gb)], [(TW, CR, CE)], "Tr")
+        for j, (a, e) in enumerate(CHUNKS):
+            n = e - a
+            zb, qb = T["z%d" % j], T["q%d" % j]
+            Z, Q = "z%d" % j, "q%d" % j
+            pn = "ps%d" % BANKS[j][0]
+            pb = T[pn]
+            SG(16 * n, lambda a=a, e=e, zb=zb: sc.activation(zb[:], T.Cc[:, 0:W].indirect(T.su[:, a:e]), F.Copy), [("Cc", 0, W), ("su", a, e)], [full(Z)], name="G2_%d" % j)
+            V(8 * n, lambda n=n, zb=zb, qb=qb: v.tensor_tensor_scan(qb[:], T.mask[:, 0:16 * n], zb[:], 0.0, A.mult, A.max), [full("mask"), full(Z)], [full(Q)], "scan3_%d" % j)
+            V(2 * n, lambda a=a, e=e, qb=qb: v.tensor_tensor(T.Inew[:, a:e], Icb[:, a:e], qb[:, 15::16], A.max), [(IC, a, e), full(Q)], [("Inew", a, e)], "Inew%d" % j)
+            V(2 * n, lambda a=a, e=e: v.tensor_tensor(T.R[:, a:e], T.Inew[:, a:e], TWb[:, CT + a:CT + e], A.is_ge), [("Inew", a, e), (TW, CT + a, CT + e)], [("R", a, e)], "R%d" % j)
+
+            def votes(a=a, e=e, n=n, pb=pb):
+                for k, (w, h) in enumerate((("bP", "hP"), ("bQ", "hQ"))):
+                    o = pb[:, k * n:k * n + n]
+                    te.matmul(o, T[w][:], T.R[:, a:e], True, False)
+                    r = te.matmul(o, T[h][0:1, :], T.one[0:1, 0:n], False, True)
+                return r
+
+            op("P", ("mm", 4), votes, [full("bP"), full("bQ"), full("hP"), full("hQ"), full("one"), ("R", a, e)], [full(pn)], name="vote%d" % j)
+            V(n, lambda a=a, e=e, n=n, pb=pb: v.tensor_tensor(T.s1[:, a:e], T.Rld[:, a:e], pb[:, 0:n], A.min), [("Rld", a, e), full(pn)], [("s1", a, e)], "s1")
+            V(n, lambda a=a, e=e, n=n, pb=pb: v.tensor_tensor(T.s2[:, a:e], T.Inew[:, a:e], pb[:, n:2 * n], A.min), [("Inew", a, e), full(pn)], [("s2", a, e)], "s2")
+            V(2 * n, lambda a=a, e=e: v.tensor_tensor(IPb[:, a:e], T.s1[:, a:e], T.s2[:, a:e], A.max), [("s1", a, e), ("s2", a, e)], [(IP, a, e)], "IP%d" % j)
+            nm = "a%d_%d" % (t, j)
+            i = op("G", ("send", 1), lambda a=a, e=e, nm=nm: send(T["Ic%d" % (t + 1)][:, a:e], IPb[:, a:e], nm), [(IP, a, e)], [], kind="send", name="A%d" % j)
+            op("X", ("net", 1), None, [], [("Ic%d" % (t + 1), a, e)], sem=(nm, ne), kind="arr", deps=[i], name="arrA%d" % j)
+        cn = "ps%d" % CB
+        pc = T[cn]
+
+        def count():
+            for p in range(16):
+                r = te.matmul(pc[:, 0:NQ], T.e3[:, 15 - p:143 - p], T.R[:, p::16], p == 0, p == 15)
+            return r
+
+        op("P", ("mm", 16), count, [full("e3"), full("R")], [full(cn)], name="count")
+        lo = 28 if last else 0
+        for k in range(lo, 42, 14):
+            V(NQ, lambda k=k: v.tensor_scalar(T.m3[:, k:k + 14], pc[:, 0:NQ], 3.5, None, A.is_ge), [full(cn)], [("m3", k, k + 14)])
+        V(42, lambda: v.tensor_tensor(T.pm[:, lo:42], T.m3[:, lo:42], T.AA[:, lo:42], A.mult), [("m3", lo, 42), ("AA", lo, 42)], [("pm", lo, 42)])
+        V(42, lambda: v.tensor_tensor(MSb[:, 4 + lo:46], T.pm[:, lo:42], TWb[:, 4 + lo:46], A.add), [("pm", lo, 42), (TW, 4 + lo, 46)], [(MS, 4 + lo, 46)])
+        if not last:
+            V(28, lambda: v.tensor_copy(T.lst[:], MSb[:, 4:32]), [(MS, 4, 32)], [full("lst")])
+            SG(M, lambda: sc.activation(MSb[:, CT:CR], TWb[:, CT:CE].indirect(T.lst[:, 14:28]), F.Copy), [(TW, CT, CE), full("lst")], [(MS, CT, CR)], name="Tsel")
+            op("V", ("scatter", M), lambda: v.tensor_copy(T.Cc[:].indirect(T.lst[:, 0:14]), T.Inew[:]), [full("Inew"), full("lst")], [full("Cc")], name="scatter")
+        hi = CT if last else CR
+        i = op("G", ("send", 1), lambda: send(T["TW%d" % (t + 1)][:, CW:hi], MSb[:, CW:hi], "b%d" % t), [(MS, CW, hi)], [], kind="send", name="B")
+        op("X", ("net", 1), None, [], [("TW%d" % (t + 1), CW, hi)], sem=("b%d" % t, ne), kind="arr", deps=[i], name="arrB")
+
+    for t in range(ST):
+        step(t)
+    IC, TW = "Ic%d" % ST, "TW%d" % ST
+    Fb = T[IC]
+    for j, (a, e) in enumerate(CHUNKS):
+        n = e - a
+        S(n, lambda a=a, e=e: sc.activation(T.lnI[:, a:e], Fb[:, a:e], F.Ln, scale=UP), [(IC, a, e)], [("lnI", a, e)], name="lnY")
+        V(n, lambda a=a, e=e: v.tensor_scalar(T.yint[:, a:e], T.lnI[:, a:e], SC, OFF, A.mult, A.add), [("lnI", a, e)], [("yint", a, e)])
+        V(n, lambda a=a, e=e: v.tensor_copy(T.yout[:, a:e], T.yint[:, a:e]), [("yint", a, e)], [("yout", a, e)])
+        op("Y", ("st", 1), lambda a=a, e=e: sy.dma_start(T.yi[:, a:e], T.yout[:, a:e]), [("yout", a, e)], [], sem="st%d" % j, kind="dma", name="yi")
+    op("Y", ("st", 1), lambda: sy.dma_start(T.yc[:], T["TW%d" % ST][:, CW:CW + NQ]), [(TW, CW, CW + NQ)], [], sem="st%d" % NC, kind="dma", name="yc")
+    return ops, nloc
+
+
+SEMOF = {"V": "vec", "S": "act", "P": "ten", "G": "gps"}
+
+
+def emit(g, T, ops, order):
+    eng = {"V": g.vector, "S": g.scalar, "P": g.tensor, "G": g, "Y": g.sync}
+    cnt = {"vec": 0, "act": 0, "ten": 0, "gps": 0}
+    seen = {q: {} for q in eng}
+    tok = {}
+    for i in order:
+        o = ops[i]
+        if o["q"] == "X":
+            tok[i] = (o["sem"][0], o["sem"][1], {o["sem"][0]: o["sem"][1]})
+            continue
+        q = o["q"]
+        s = seen[q]
+        toks = sorted([tok[d] for d in o["deps"] if tok.get(d) is not None], key=lambda x: (-sum(x[2].values()), x[0]))
+        top = {}
+        for sem, val, clock in toks:
+            top[sem] = max(top.get(sem, 0), val)
+        for sem, val, clock in toks:
+            if s.get(sem, 0) >= val or top[sem] > val:
+                continue
+            eng[q].wait_ge(T.sem[sem], val)
+            for k, w in clock.items():
+                s[k] = max(s.get(k, 0), w)
+        r = o["fn"]()
+        tok[i] = None
+        if o["kind"] == "c":
+            sem = SEMOF[q]
+            cnt[sem] += 1
+            r.then_inc(T.sem[sem], 1)
+            c = dict(s)
+            c[sem] = cnt[sem]
+            tok[i] = (sem, cnt[sem], c)
+        elif o["kind"] == "dma":
+            r.then_inc(T.sem[o["sem"]], 16)
+    for sem in sorted(cnt):
+        g.wait_ge(T.sem[sem], cnt[sem])
+
+
+def rank_program(g, core, T, topo):
+    rank = T.rank_of(core)
+    if rank is None:
+        return
+    ops, nloc = build(g, T, topo, core, rank)
+    order, beg, fin = plan(ops)
+    emit(g, T, ops, order)
+    for k in range(NC + 1):
+        g.wait_ge(T.sem["st%d" % k], 16)
+    g.wait_ge(T.sem.loc, nloc[0])

@@ -6,15 +6,15 @@ W = 3584
 M = 224
 ST = 4
 NQ = 14
-SIZES = [64, 64, 48, 48]
+SIZES = [64, 64, 64, 32]
 CHUNKS = []
 _a = 0
 for _n in SIZES:
     CHUNKS.append((_a, _a + _n))
     _a += _n
 NC = len(CHUNKS)
-PIECES = 4
-PW = W // PIECES
+CP = [(16 * _x, 16 * _y) for _x, _y in CHUNKS]
+LP = [(896 * _x, 896 * _x + 896) for _x in range(4)]
 KE = 512.0
 KV = float(2 ** 60)
 SC = 32.0 / math.log(2.0)
@@ -34,21 +34,21 @@ def _declare():
 
     sb("ck32 la32", W, "int32")
     sb("cf lf", W, "float32")
-    sb("Cc", W + M, "bfloat16")
+    sb("Cc", 2 * W, "bfloat16")
     sb("Lc", W, "bfloat16")
-    sb("cu32 il32 nx nxa rl32 pt pa q16 cl c16", NQ, "int32")
+    sb("cu32 il32 rl32 pt pa q16 cl c16", NQ, "int32")
+    sb("ni nw", 28, "int32")
     sb("gap32 yint", M, "int32")
     sb("gapf gc0 gc1 gc2 lnI lnS yout", M, "float32")
     sb("il rl", NQ, "uint16")
     sb("Iu su", M, "uint16")
-    sb("Inew Rld R s1 s2", M, "bfloat16")
-    sb("AA m3 pm", 42, "float32")
-    sb("c15", NQ, "float32")
+    sb("Inew Rld R s2", M, "bfloat16")
+    sb("pm", 42, "float32")
     sb("lst", 28, "uint16")
     sb("mask", 1024, "bfloat16")
-    sb("fK fN idK idN fP fQ bP1 bP bQ1 bQ hP hQ", 128, "bfloat16")
+    sb("fK fN idK idN fP fQ bP1 bP bQ1 bQ hP hQ f1 id1", 128, "bfloat16")
+    sb("fF idF", 128, "float32")
     sb("fE e1 e2 e3", 144, "bfloat16")
-    sb("one", 64, "bfloat16")
     for t in range(ST + 1):
         sb("Ic%d" % t, M, "bfloat16")
         sb("TW%d" % t, CE, "float32")
@@ -66,17 +66,21 @@ BANKS = []
 _b = 0
 for _n in SIZES:
     _k = -(-_n * 16 // 512)
-    BANKS.append(list(range(_b, _b + _k)))
+    BANKS.append([(_b + _i) % 8 for _i in range(_k)])
     _b += _k
-CB = min(_b, 7)
+CB = 7
 
 SEMAPHORES = ["vec", "act", "ten", "gps", "loc", "gap"]
 for _t in range(ST):
     SEMAPHORES += ["a%d_%d" % (_t, _j) for _j in range(NC)] + ["b%d" % _t]
-SEMAPHORES += ["ld%d" % _k for _k in range(2 * PIECES + 2)] + ["st%d" % _k for _k in range(NC + 1)]
+SEMAPHORES += ["ld%d" % _k for _k in range(len(CP) + len(LP) + 2)] + ["st%d" % _k for _k in range(NC + 1)]
 
-COST = {"cy": 0.83e-3 * 1.25, "gather": 1.56, "scatter": 3.8, "fix": 0.03, "gfix": 0.07, "lat": 0.08, "net": 2.2, "send": 0.9,
-        "mm": 0.046 * 1.25, "ld0": 2.0, "ld": 2.3, "st": 2.0}
+COST = {"cy": 0.83e-3, "gather": 1.4, "scatter": 3.0, "fix": 0.03, "gfix": 0.07, "lat": 0.05, "net": 2.0, "send": 0.9,
+        "mm": 0.046, "ld0": 2.0, "ld": 1.4, "tab": 1.5}
+NUDGE = {}
+for _w in ("scan2_2:-6 min1_0:-1 lnS2:-5 diff1_1:7 scan3_3:5 lnS0:5 diff2_0:-5 min3_0:-2 scan3_1:-4 s2_0:2 gapc:6 vote2:8 min2_1:-7 G1_2:-6 min1_1:8 "
+           "count:7 n3:2 n4:-2 scan2_3:-2 G2_1:-7 n1:6 decS0:1 s1_0:2 Iu0:-5 scan3_0:-3 Tr:-6").split():
+    NUDGE[_w.split(":")[0]] = float(_w.split(":")[1])
 
 
 def dur(ck, c):
@@ -85,6 +89,8 @@ def dur(ck, c):
         return c["fix"] + max(64, n) * c["cy"]
     if k == "s":
         return c["gfix"] + max(32, n) * c["cy"]
+    if k == "stab":
+        return c["tab"] + c["gfix"] + n * c["cy"]
     if k == "gather":
         return c["gfix"] + n * c["gather"] * c["cy"]
     if k == "scatter":
@@ -100,7 +106,7 @@ def dur(ck, c):
     return n * c[k]
 
 
-def plan(ops, c=COST, jit=None):
+def plan(ops, c=COST, nudge=NUDGE):
     n = len(ops)
     cost = [dur(o["ck"], c) for o in ops]
     lat = c["lat"]
@@ -114,8 +120,7 @@ def plan(ops, c=COST, jit=None):
         for k in succ[i]:
             best = max(best, prio[k] + lat)
         prio[i] = cost[i] + best
-    if jit:
-        prio = [p + j for p, j in zip(prio, jit)]
+    prio = [p + nudge.get(o["name"], 0.0) for p, o in zip(prio, ops)]
     left = [len(o["deps"]) for o in ops]
     est = [0.0] * n
     ready = [i for i in range(n) if left[i] == 0]
@@ -169,8 +174,8 @@ def build(g, T, topo, core, rank):
     def V(n, fn, reads, writes, name=""):
         return op("V", ("v", n), fn, reads, writes, name=name)
 
-    def S(n, fn, reads, writes, name="", deps=()):
-        return op("S", ("s", n), fn, reads, writes, name=name, deps=deps)
+    def S(n, fn, reads, writes, name="", deps=(), k="s"):
+        return op("S", (k, n), fn, reads, writes, name=name, deps=deps)
 
     def SG(n, fn, reads, writes, name=""):
         return op("S", ("gather", n), fn, reads, writes, name=name)
@@ -180,20 +185,9 @@ def build(g, T, topo, core, rank):
 
     v, sc, te, sy = g.vector, g.scalar, g.tensor, g.sync
 
-    def fill(b, n, c):
-        V(n, lambda: v.memset(T[b][:], c), [], [full(b)], "fill")
-
-    fill("fK", 64, KE)
-    fill("fN", 64, -KE)
-    fill("fP", 64, KV)
-    fill("fQ", 64, -KV)
-    fill("fE", 64, 1.0)
-    fill("hP", 64, -3.5 * KV)
-    fill("hQ", 64, 3.5 * KV)
-    fill("one", 64, 1.0)
-    fill("mask", 512, 1.0)
+    for b, c in (("fK", KE), ("fN", -KE), ("fP", KV), ("fQ", -KV), ("fE", 1.0), ("hP", -3.5 * KV), ("hQ", 3.5 * KV), ("f1", 1.0), ("fF", 1.0), ("mask", 1.0)):
+        V(512 if b == "mask" else 64, lambda b=b, c=c: v.memset(T[b][:], c), [], [full(b)], "fill")
     V(64, lambda: v.memset(T.mask[:, 0::16], 0.0), [], [full("mask")], "mask")
-    V(64, lambda: v.memset(T.AA[:, 14:28], float(M)), [], [("AA", 14, 28)], "AA")
     for t in range(ST):
         V(64, lambda t=t: v.memset(T["MS%d" % t][:, CW:CT], 0.0), [], [("MS%d" % t, CW, CT)], "MSpad")
 
@@ -202,12 +196,11 @@ def build(g, T, topo, core, rank):
 
     op("G", ("us", 0.2), lambda: g.iota(T.pt[:], [[0, NQ]], 0, 1), [], [full("pt")], name="iota")
     op("G", ("us", 0.2), lambda: g.iota(T.q16[:], [[16, NQ]], 0, 0), [], [full("q16")], name="iota")
-    sel("idK", "fK", 128, [[-1, 128]], A.is_equal, 0, 1)
-    sel("idN", "fN", 128, [[-1, 128]], A.is_equal, 0, 1)
-    sel("bP1", "fP", 128, [[-16, 8], [0, 16]], A.is_ge, 0, 1)
-    sel("bP", "bP1", 128, [[16, 8], [0, 16]], A.is_ge, 15, -1)
-    sel("bQ1", "fQ", 128, [[-16, 8], [0, 16]], A.is_ge, 0, 1)
-    sel("bQ", "bQ1", 128, [[16, 8], [0, 16]], A.is_ge, 15, -1)
+    for o, f in (("idN", "fN"), ("idK", "fK"), ("idF", "fF"), ("id1", "f1")):
+        sel(o, f, 128, [[-1, 128]], A.is_equal, 0, 1)
+    for x in "PQ":
+        sel("b" + x + "1", "f" + x, 128, [[-16, 8], [0, 16]], A.is_ge, 0, 1)
+        sel("b" + x, "b" + x + "1", 128, [[16, 8], [0, 16]], A.is_ge, 15, -1)
     sel("e1", "fE", 144, [[0, 9], [1, 16]], A.is_equal, -15, 0)
     sel("e2", "e1", 144, [[-16, 9], [0, 16]], A.is_ge, 0, 1)
     sel("e3", "e2", 144, [[16, 9], [0, 16]], A.is_ge, 15, -1)
@@ -215,42 +208,62 @@ def build(g, T, topo, core, rank):
     V(NQ, lambda: v.tensor_scalar(T.pa[:], T.pt[:], 15, None, A.bitwise_and), [full("pt")], [full("pa")])
     V(NQ, lambda: v.tensor_tensor(T.cl[:], T.pa[:], T.q16[:], A.add), [full("pa"), full("q16")], [full("cl")])
     V(NQ, lambda: v.tensor_scalar(T.c16[:], T.cl[:], 16.0, None, A.mult), [full("cl")], [full("c16")])
-    V(NQ, lambda: v.tensor_scalar(T.c15[:], T.cl[:], 15.0, float(-W), A.mult, A.add), [full("cl")], [full("c15")])
     for t in range(ST - 1):
         b = "TW%d" % t
-        V(NQ, lambda b=b: v.tensor_scalar(T[b][:, 4:18], T.cl[:], float(W), None, A.add), [full("cl")], [(b, 4, 18)])
         V(NQ, lambda b=b: v.tensor_scalar(T[b][:, 18:32], T.cl[:], 1.0, None, A.mult), [full("cl")], [(b, 18, 32)])
 
-    dq = {"sync": ("Y", sy), "act": ("S", sc)}
+    dq = {"Y": sy, "S": sc}
+    nld = [0]
+    amount = [0]
 
-    def load(which, k, out, in_, b, lo, hi, n):
-        q, e = dq[which]
-        i = op(q, ("us", 0.06), lambda: e.dma_start(out, in_), [], [], sem="ld%d" % k, kind="dma", name="ld")
-        op("X", ("ld", n), None, [], [(b, lo, hi)], sem=("ld%d" % k, 16), kind="arr", deps=[i], name="land")
+    def load(q, out, in_, b, lo, hi):
+        k = nld[0]
+        nld[0] += 1
+        amount[0] += hi - lo
+        i = op(q, ("us", 0.06), lambda: dq[q].dma_start(out, in_), [], [], sem="ld%d" % k, kind="dma", name="ld")
+        op("X", ("ld", amount[0] / 896.0), None, [], [(b, lo, hi)], sem=("ld%d" % k, 16), kind="arr", deps=[i], name="land")
 
-    load("sync", 2 * PIECES, T.cu32[:], T.cu[:], "cu32", 0, NQ, 0)
-    k = 0
-    for b, src in (("ck32", T.ck), ("la32", T.la)):
-        for p in range(PIECES):
-            lo, hi = p * PW, (p + 1) * PW
-            load("sync" if p % 2 == 0 else "act", k, T[b][:, lo:hi], src[:, lo:hi], b, lo, hi, k + 1)
-            k += 1
-        if b == "ck32":
-            load("act", 2 * PIECES + 1, T.gap32[:], T.gap[:], "gap32", 0, M, k)
+    def load_c(q, p):
+        lo, hi = CP[p]
+        load(q, T.ck32[:, lo:hi], T.ck[:, lo:hi], "ck32", lo, hi)
+
+    def load_l(q, p):
+        lo, hi = LP[p]
+        load(q, T.la32[:, lo:hi], T.la[:, lo:hi], "la32", lo, hi)
+
+    load("Y", T.cu32[:], T.cu[:], "cu32", 0, NQ)
+    load_c("Y", 0)
+    load_l("S", 0)
+    load_l("Y", 1)
+    load_l("S", 2)
+    load_l("Y", 3)
+    load_c("S", 1)
+    load("Y", T.gap32[:], T.gap[:], "gap32", 0, M)
+    load_c("S", 2)
+    load_c("Y", 3)
 
     V(NQ, lambda: v.tensor_copy(T.TW0[:, CW:CW + NQ], T.cu32[:]), [full("cu32")], [("TW0", CW, CW + NQ)])
     V(NQ, lambda: v.tensor_tensor(T.il32[:], T.cu32[:], T.c16[:], A.add), [full("cu32"), full("c16")], [full("il32")])
     V(NQ, lambda: v.tensor_copy(T.il[:], T.il32[:]), [full("il32")], [full("il")])
-    op("V", ("gather", M), lambda: v.tensor_copy(T.Iu[:], T.ck32[:].indirect(T.il[:])), [full("ck32"), full("il")], [full("Iu")], name="Iu0")
-    lastexp = []
-    for b, f, o in (("ck32", "cf", "Cc"), ("la32", "lf", "Lc")):
-        for p in range(PIECES):
-            lo, hi = p * PW, (p + 1) * PW
-            V(PW, lambda b=b, f=f, lo=lo, hi=hi: v.tensor_copy(T[f][:, lo:hi], T[b][:, lo:hi]), [(b, lo, hi)], [(f, lo, hi)], "conv")
-            lastexp.append(S(PW, lambda f=f, o=o, lo=lo, hi=hi: sc.activation(T[o][:, lo:hi], T[f][:, lo:hi], F.Exp, bias=B0, scale=1.0 / SC),
-                             [(f, lo, hi)], [(o, lo, hi)], name="exp"))
+    for a, e in CHUNKS:
+        op("V", ("gather", e - a), lambda a=a, e=e: v.tensor_copy(T.Iu[:, a:e], T.ck32[:, 0:16 * e].indirect(T.il[:, a // 16:e // 16])),
+           [("ck32", 0, 16 * e), full("il")], [("Iu", a, e)], name="Iu0")
+    exps = []
+
+    def encode(src, f, o, lo, hi, q, k="s"):
+        if q == "V":
+            V(hi - lo, lambda: v.tensor_copy(T[f][:, lo:hi], T[src][:, lo:hi]), [(src, lo, hi)], [(f, lo, hi)], "conv")
+        else:
+            op("G", ("sel", hi - lo), lambda: g.affine_select(T[f][:, lo:hi], T[src][:, lo:hi], [[0, hi - lo]], A.is_ge, 0.0, 0, 0), [(src, lo, hi)], [(f, lo, hi)], name="convg")
+        exps.append(S(hi - lo, lambda: sc.activation(T[o][:, lo:hi], T[f][:, lo:hi], F.Exp, bias=B0, scale=1.0 / SC), [(f, lo, hi)], [(o, lo, hi)], name="exp", k=k))
+
+    encode("ck32", "cf", "Cc", CP[0][0], CP[0][1], "V", "stab")
+    for lo, hi in LP:
+        encode("la32", "lf", "Lc", lo, hi, "V")
+    for lo, hi in CP[1:]:
+        encode("ck32", "cf", "Cc", lo, hi, "G")
     V(M, lambda: v.tensor_scalar(T.gapf[:], T.gap32[:], 0.5, None, A.subtract), [full("gap32")], [full("gapf")])
-    lastexp.append(S(M, lambda: sc.activation(T.gc0[:], T.gapf[:], F.Exp, scale=1.0 / SC), [full("gapf")], [full("gc0")], name="expg"))
+    exps.append(S(M, lambda: sc.activation(T.gc0[:], T.gapf[:], F.Exp, scale=1.0 / SC), [full("gapf")], [full("gc0")], name="expg"))
 
     nloc = [0]
     cores = list(T.cores)
@@ -278,13 +291,19 @@ def build(g, T, topo, core, rank):
         nloc[0] += ne
         g.remote_dma(out, in_, T.sem[sem], T.sem.loc, a[1], a[0], topo.mask(core, nxt))
 
+    cn = "ps%d" % CB
+    pc = T[cn]
     SG(M, lambda: sc.activation(T.Ic0[:], T.Cc[:, 0:W].indirect(T.il[:]), F.Copy), [("Cc", 0, W), full("il")], [full("Ic0")], name="Ic0")
-    V(2 * M, lambda: v.tensor_tensor(T.TW0[:, CT:CR], T.Ic0[:], T.gc0[:], A.mult), [full("Ic0"), full("gc0")], [("TW0", CT, CR)], "Tc0")
 
     def step(t):
         last = t == ST - 1
         IC, TW, MS, IP = "Ic%d" % t, "TW%d" % t, "MS%d" % t, "IP%d" % t
         Icb, TWb, MSb, IPb = T[IC], T[TW], T[MS], T[IP]
+        if not last:
+            gb = "gc%d" % t
+            op("P", ("mm", 14), lambda: te.matmul(pc[:, 16:240], T.idF[:], T[gb][:], True, True), [full("idF"), full(gb)], [full(cn)], name="gapc")
+            if t == 0:
+                V(M, lambda: v.tensor_tensor(TWb[:, CT:CR], T.Ic0[:], pc[:, 16:240], A.mult), [full("Ic0"), full(cn)], [("TW0", CT, CR)], "Tc0")
         for j, (a, e) in enumerate(CHUNKS):
             n = e - a
             xb, yb, Pb, ub = T["x%d" % j], T["y%d" % j], T["P%d" % j], T["u%d" % j]
@@ -296,60 +315,61 @@ def build(g, T, topo, core, rank):
             V(8 * n, lambda n=n, xb=xb, Pb=Pb: v.tensor_tensor_scan(Pb[:], T.mask[:, 0:16 * n], xb[:], 0.0, A.mult, A.max), [full("mask"), full(X)], [full(P)], "scan1_%d" % j)
             bk = BANKS[j]
             per = 16 // len(bk)
-
-            def diff(n=n, xb=xb, Pb=Pb, bk=bk, per=per):
-                for h, b in enumerate(bk):
-                    te.matmul(T["ps%d" % b][:, 0:per * n], T.idN[:], xb[:, h::len(bk)], True, False)
-                    for i in range(per):
-                        r = te.matmul(T["ps%d" % b][:, i:per * n:per], T.idK[:], Pb[:, 15::16], False, i == per - 1)
-                return r
-
-            op("P", ("mm", 16 + 16 * n / 64), diff, [full("idK"), full("idN"), full(P), full(X)], [full("ps%d" % b) for b in bk], name="diff%d" % j)
             for h, b in enumerate(bk):
-                V(per * n, lambda n=n, xb=xb, yb=yb, h=h, b=b, per=per, bk=bk: v.tensor_tensor(yb[:, h::len(bk)], xb[:, h::len(bk)], T["ps%d" % b][:, 0:per * n], A.min),
+                def diff(n=n, xb=xb, Pb=Pb, h=h, k=len(bk), per=per, pb=T["ps%d" % b]):
+                    te.matmul(pb[:, 0:per * n], T.idN[:], xb[:, h::k], True, False)
+                    for i in range(per):
+                        r = te.matmul(pb[:, i:per * n:per], T.idK[:], Pb[:, 15::16], False, i == per - 1)
+                    return r
+
+                op("P", ("mm", per + per * n / 64), diff, [full("idK"), full("idN"), full(P), full(X)], [full("ps%d" % b)], name="diff%d_%d" % (j, h))
+                V(per * n, lambda n=n, xb=xb, yb=yb, h=h, k=len(bk), per=per, pb=T["ps%d" % b]: v.tensor_tensor(yb[:, h::k], xb[:, h::k], pb[:, 0:per * n], A.min),
                   [full(X), full("ps%d" % b)], [(Y, h, h + 1)], "min%d_%d" % (j, h))
             V(8 * n, lambda n=n, yb=yb, ub=ub: v.tensor_tensor_scan(ub[:], T.mask[:, 0:16 * n], yb[:], 0.0, A.mult, A.max), [full("mask"), full(Y)], [full(U)], "scan2_%d" % j)
             S(n, lambda a=a, e=e, ub=ub: sc.activation(T.lnS[:, a:e], ub[:, 15::16], F.Ln, bias=EPS, scale=UP), [full(U)], [("lnS", a, e)],
-              deps=lastexp if t == 0 else (), name="lnS%d" % j)
+              deps=exps if t == 0 else (), name="lnS%d" % j, k="stab" if t == 0 and j == 0 else "s")
             V(n, lambda a=a, e=e: v.tensor_scalar(T.su[:, a:e], T.lnS[:, a:e], SC, OFF + 0.25, A.mult, A.add), [("lnS", a, e)], [("su", a, e)], "decS%d" % j)
-        V(NQ, lambda: v.tensor_scalar(T.nxa[:], TWb[:, CW:CW + NQ], 1.0, None, A.add), [(TW, CW, CW + NQ)], [full("nxa")])
-        V(NQ, lambda: v.tensor_scalar(T.nx[:], T.nxa[:], 15, None, A.bitwise_and), [full("nxa")], [full("nx")])
-        V(NQ, lambda: v.tensor_tensor(T.rl32[:], T.nx[:], T.c16[:], A.add), [full("nx"), full("c16")], [full("rl32")])
-        V(NQ, lambda: v.tensor_copy(T.rl[:], T.rl32[:]), [full("rl32")], [full("rl")])
-        V(NQ, lambda: v.tensor_tensor(T.AA[:, 28:42], T.nx[:], TWb[:, CW:CW + NQ], A.subtract), [full("nx"), (TW, CW, CW + NQ)], [("AA", 28, 42)])
+        V(NQ, lambda: v.tensor_copy(T.ni[:, 0:14], TWb[:, CW:CW + NQ]), [(TW, CW, CW + NQ)], [("ni", 0, 14)], "n0")
+        V(NQ, lambda: v.tensor_scalar(T.ni[:, 14:28], TWb[:, CW:CW + NQ], 1.0, None, A.add), [(TW, CW, CW + NQ)], [("ni", 14, 28)], "n1")
+        V(NQ, lambda: v.tensor_scalar(T.nw[:], T.ni[:], 15, None, A.bitwise_and), [full("ni")], [full("nw")], "n2")
+        V(NQ, lambda: v.tensor_tensor(T.rl32[:], T.nw[:, 14:28], T.c16[:], A.add), [full("nw"), full("c16")], [full("rl32")], "n3")
+        V(NQ, lambda: v.tensor_copy(T.rl[:], T.rl32[:]), [full("rl32")], [full("rl")], "n4")
         if not last:
-            V(NQ, lambda: v.tensor_tensor(T.AA[:, 0:14], T.c15[:], TWb[:, CW:CW + NQ], A.add), [full("c15"), (TW, CW, CW + NQ)], [("AA", 0, 14)])
+            V(NQ, lambda: v.tensor_tensor(TWb[:, 4:18], T.nw[:, 0:14], T.c16[:], A.add), [full("nw"), full("c16")], [(TW, 4, 18)], "n5")
         SG(M, lambda: sc.activation(T.Rld[:], T.Cc[:, 0:W].indirect(T.rl[:]), F.Copy), [("Cc", 0, W), full("rl")], [full("Rld")], name="Rld")
         if not last:
-            gb = "gc%d" % t
-            V(2 * M, lambda: v.tensor_tensor(TWb[:, CR:CE], T.Rld[:], T[gb][:], A.mult), [full("Rld"), full(gb)], [(TW, CR, CE)], "Tr")
+            V(M, lambda: v.tensor_tensor(TWb[:, CR:CE], T.Rld[:], pc[:, 16:240], A.mult), [full("Rld"), full(cn)], [(TW, CR, CE)], "Tr")
         for j, (a, e) in enumerate(CHUNKS):
             n = e - a
             zb, qb = T["z%d" % j], T["q%d" % j]
             Z, Q = "z%d" % j, "q%d" % j
-            pn = "ps%d" % BANKS[j][0]
-            pb = T[pn]
+            pn, qn = "ps%d" % BANKS[j][0], "ps%d" % BANKS[j][-1]
+            pb, qp = T[pn], T[qn]
+
+            def prep(a=a, e=e, n=n, qp=qp):
+                te.matmul(qp[:, 256:256 + n], T.id1[:], Icb[:, a:e], True, True)
+                return te.matmul(qp[:, 320:320 + n], T.idF[:], TWb[:, CT + a:CT + e], True, True)
+
+            op("P", ("mm", 5), prep, [full("id1"), full("idF"), (IC, a, e), (TW, CT + a, CT + e)], [full(qn)], name="prep%d" % j)
             SG(16 * n, lambda a=a, e=e, zb=zb: sc.activation(zb[:], T.Cc[:, 0:W].indirect(T.su[:, a:e]), F.Copy), [("Cc", 0, W), ("su", a, e)], [full(Z)], name="G2_%d" % j)
             V(8 * n, lambda n=n, zb=zb, qb=qb: v.tensor_tensor_scan(qb[:], T.mask[:, 0:16 * n], zb[:], 0.0, A.mult, A.max), [full("mask"), full(Z)], [full(Q)], "scan3_%d" % j)
-            V(2 * n, lambda a=a, e=e, qb=qb: v.tensor_tensor(T.Inew[:, a:e], Icb[:, a:e], qb[:, 15::16], A.max), [(IC, a, e), full(Q)], [("Inew", a, e)], "Inew%d" % j)
-            V(2 * n, lambda a=a, e=e: v.tensor_tensor(T.R[:, a:e], T.Inew[:, a:e], TWb[:, CT + a:CT + e], A.is_ge), [("Inew", a, e), (TW, CT + a, CT + e)], [("R", a, e)], "R%d" % j)
+            V(n, lambda a=a, e=e, n=n, qb=qb, qp=qp: v.tensor_tensor(T.Inew[:, a:e], qb[:, 15::16], qp[:, 256:256 + n], A.max), [full(qn), full(Q)], [("Inew", a, e)], "Inew%d" % j)
+            V(n, lambda a=a, e=e, n=n, qp=qp: v.tensor_tensor(T.R[:, a:e], T.Inew[:, a:e], qp[:, 320:320 + n], A.is_ge), [("Inew", a, e), full(qn)], [("R", a, e)], "R%d" % j)
 
             def votes(a=a, e=e, n=n, pb=pb):
                 for k, (w, h) in enumerate((("bP", "hP"), ("bQ", "hQ"))):
                     o = pb[:, k * n:k * n + n]
                     te.matmul(o, T[w][:], T.R[:, a:e], True, False)
-                    r = te.matmul(o, T[h][0:1, :], T.one[0:1, 0:n], False, True)
+                    r = te.matmul(o, T[h][0:1, :], T.f1[0:1, 0:n], False, True)
                 return r
 
-            op("P", ("mm", 4), votes, [full("bP"), full("bQ"), full("hP"), full("hQ"), full("one"), ("R", a, e)], [full(pn)], name="vote%d" % j)
-            V(n, lambda a=a, e=e, n=n, pb=pb: v.tensor_tensor(T.s1[:, a:e], T.Rld[:, a:e], pb[:, 0:n], A.min), [("Rld", a, e), full(pn)], [("s1", a, e)], "s1")
-            V(n, lambda a=a, e=e, n=n, pb=pb: v.tensor_tensor(T.s2[:, a:e], T.Inew[:, a:e], pb[:, n:2 * n], A.min), [("Inew", a, e), full(pn)], [("s2", a, e)], "s2")
-            V(2 * n, lambda a=a, e=e: v.tensor_tensor(IPb[:, a:e], T.s1[:, a:e], T.s2[:, a:e], A.max), [("s1", a, e), ("s2", a, e)], [(IP, a, e)], "IP%d" % j)
+            op("P", ("mm", 4), votes, [full("bP"), full("bQ"), full("hP"), full("hQ"), full("f1"), ("R", a, e)], [full(pn)], name="vote%d" % j)
+            V(n, lambda a=a, e=e, n=n, pb=pb: v.tensor_tensor(T.s2[:, a:e], T.Inew[:, a:e], pb[:, n:2 * n], A.min), [("Inew", a, e), full(pn)], [("s2", a, e)], "s2_%d" % j)
+            V(n, lambda a=a, e=e, n=n, pb=pb: v.tensor_tensor(pb[:, 128:128 + n], T.Rld[:, a:e], pb[:, 0:n], A.min), [("Rld", a, e), full(pn)], [full(pn)], "s1_%d" % j)
+            V(n, lambda a=a, e=e, n=n, pb=pb: v.tensor_tensor(IPb[:, a:e], T.s2[:, a:e], pb[:, 128:128 + n], A.max), [full(pn), ("s2", a, e)], [(IP, a, e)], "IP%d" % j)
             nm = "a%d_%d" % (t, j)
             i = op("G", ("send", 1), lambda a=a, e=e, nm=nm: send(T["Ic%d" % (t + 1)][:, a:e], IPb[:, a:e], nm), [(IP, a, e)], [], kind="send", name="A%d" % j)
             op("X", ("net", 1), None, [], [("Ic%d" % (t + 1), a, e)], sem=(nm, ne), kind="arr", deps=[i], name="arrA%d" % j)
-        cn = "ps%d" % CB
-        pc = T[cn]
 
         def count():
             for p in range(16):
@@ -358,12 +378,13 @@ def build(g, T, topo, core, rank):
 
         op("P", ("mm", 16), count, [full("e3"), full("R")], [full(cn)], name="count")
         lo = 28 if last else 0
-        for k in range(lo, 42, 14):
-            V(NQ, lambda k=k: v.tensor_scalar(T.m3[:, k:k + 14], pc[:, 0:NQ], 3.5, None, A.is_ge), [full(cn)], [("m3", k, k + 14)])
-        V(42, lambda: v.tensor_tensor(T.pm[:, lo:42], T.m3[:, lo:42], T.AA[:, lo:42], A.mult), [("m3", lo, 42), ("AA", lo, 42)], [("pm", lo, 42)])
-        V(42, lambda: v.tensor_tensor(MSb[:, 4 + lo:46], T.pm[:, lo:42], TWb[:, 4 + lo:46], A.add), [("pm", lo, 42), (TW, 4 + lo, 46)], [(MS, 4 + lo, 46)])
         if not last:
-            V(28, lambda: v.tensor_copy(T.lst[:], MSb[:, 4:32]), [(MS, 4, 32)], [full("lst")])
+            V(NQ, lambda: v.tensor_scalar(T.pm[:, 0:14], pc[:, 0:NQ], 3.5, float(W), A.is_lt, A.mult), [full(cn)], [("pm", 0, 14)], "c0")
+            V(NQ, lambda: v.tensor_scalar(T.pm[:, 14:28], pc[:, 0:NQ], 3.5, float(M), A.is_ge, A.mult), [full(cn)], [("pm", 14, 28)], "c1")
+        V(NQ, lambda: v.tensor_scalar(T.pm[:, 28:42], pc[:, 0:NQ], 3.5, None, A.is_ge), [full(cn)], [("pm", 28, 42)], "c2")
+        V(42, lambda: v.tensor_tensor(MSb[:, 4 + lo:46], T.pm[:, lo:42], TWb[:, 4 + lo:46], A.add), [("pm", lo, 42), (TW, 4 + lo, 46)], [(MS, 4 + lo, 46)], "c3")
+        if not last:
+            V(28, lambda: v.tensor_copy(T.lst[:], MSb[:, 4:32]), [(MS, 4, 32)], [full("lst")], "c4")
             SG(M, lambda: sc.activation(MSb[:, CT:CR], TWb[:, CT:CE].indirect(T.lst[:, 14:28]), F.Copy), [(TW, CT, CE), full("lst")], [(MS, CT, CR)], name="Tsel")
             op("V", ("scatter", M), lambda: v.tensor_copy(T.Cc[:].indirect(T.lst[:, 0:14]), T.Inew[:]), [full("Inew"), full("lst")], [full("Cc")], name="scatter")
         hi = CT if last else CR
@@ -373,14 +394,17 @@ def build(g, T, topo, core, rank):
     for t in range(ST):
         step(t)
     IC, TW = "Ic%d" % ST, "TW%d" % ST
-    Fb = T[IC]
+    Fb, Lb = T[IC], T[TW]
     for j, (a, e) in enumerate(CHUNKS):
         n = e - a
         S(n, lambda a=a, e=e: sc.activation(T.lnI[:, a:e], Fb[:, a:e], F.Ln, scale=UP), [(IC, a, e)], [("lnI", a, e)], name="lnY")
         V(n, lambda a=a, e=e: v.tensor_scalar(T.yint[:, a:e], T.lnI[:, a:e], SC, OFF, A.mult, A.add), [("lnI", a, e)], [("yint", a, e)])
         V(n, lambda a=a, e=e: v.tensor_copy(T.yout[:, a:e], T.yint[:, a:e]), [("yint", a, e)], [("yout", a, e)])
-        op("Y", ("st", 1), lambda a=a, e=e: sy.dma_start(T.yi[:, a:e], T.yout[:, a:e]), [("yout", a, e)], [], sem="st%d" % j, kind="dma", name="yi")
-    op("Y", ("st", 1), lambda: sy.dma_start(T.yc[:], T["TW%d" % ST][:, CW:CW + NQ]), [(TW, CW, CW + NQ)], [], sem="st%d" % NC, kind="dma", name="yc")
+        op("Y", ("us", 0.1), lambda a=a, e=e: sy.dma_start(T.yi[:, a:e], T.yout[:, a:e]), [("yout", a, e)], [], sem="st%d" % j, kind="dma", name="yi")
+    V(NQ, lambda: v.tensor_copy(T.ni[:, 0:14], Lb[:, CW:CW + NQ]), [(TW, CW, CW + NQ)], [("ni", 0, 14)])
+    V(NQ, lambda: v.tensor_scalar(T.nw[:, 0:14], T.ni[:, 0:14], 15, None, A.bitwise_and), [("ni", 0, 14)], [("nw", 0, 14)])
+    V(NQ, lambda: v.tensor_copy(Lb[:, 4:18], T.nw[:, 0:14]), [("nw", 0, 14)], [(TW, 4, 18)])
+    op("Y", ("us", 0.1), lambda: sy.dma_start(T.yc[:], Lb[:, 4:18]), [(TW, 4, 18)], [], sem="st%d" % NC, kind="dma", name="yc")
     return ops, nloc
 
 

import math
from concourse.bass import DstId, RemoteDMATransfer
from concourse.mybir import dt, AluOpType, AxisListType, ActivationFunctionType

W = 3584
M = 224
ST = 4
NQ = 14
SIZES = [64, 64, 64, 32]
CHUNKS = []
_a = 0
for _n in SIZES:
    CHUNKS.append((_a, _a + _n))
    _a += _n
NC = len(CHUNKS)
CP = [(16 * _x, 16 * _y) for _x, _y in CHUNKS]
LP = [(896 * _x, 896 * _x + 896) for _x in range(4)]
KE = 512.0
KV = float(2 ** 60)
SC = 32.0 / math.log(2.0)
B0 = -100.0 * math.log(2.0)
UP = 2.0 ** 50
OFF = 1600.0
EPS = 2.0 ** -62
CW, CT, CR, CE = 32, 48, 272, 496

SCRATCH = {}


def _declare():
    def sb(names, n, t):
        for x in names.split():
            SCRATCH[x] = ("sbuf", [128, n], t)

    sb("ck32 la32", W, "int32")
    sb("cf lf", W, "float32")
    sb("Cc", 2 * W, "bfloat16")
    sb("Lc", W, "bfloat16")
    sb("cu32 il32 rl32 pt pa q16 cl c16", NQ, "int32")
    sb("ni nw", 28, "int32")
    sb("gap32 yint", M, "int32")
    sb("gapf gc0 gc1 gc2 lnI lnS yout", M, "float32")
    sb("il rl", NQ, "uint16")
    sb("Iu su", M, "uint16")
    sb("Inew Rld R s2", M, "bfloat16")
    sb("pm", 42, "float32")
    sb("lst", 28, "uint16")
    sb("mask", 1024, "bfloat16")
    sb("fK fN idK idN fP fQ bP1 bP bQ1 bQ hP hQ f1 id1", 128, "bfloat16")
    sb("fF idF", 128, "float32")
    sb("fE e1 e2 e3", 144, "bfloat16")
    for t in range(ST + 1):
        sb("Ic%d" % t, M, "bfloat16")
        sb("TW%d" % t, CE, "float32")
    for t in range(ST):
        sb("MS%d" % t, CR, "float32")
        sb("IP%d" % t, M, "bfloat16")
    for j, n in enumerate(SIZES):
        sb("x%d y%d P%d u%d z%d q%d" % (j, j, j, j, j, j), n * 16, "bfloat16")
    for k in range(8):
        SCRATCH["ps%d" % k] = ("psum", [128, 512], "float32")


_declare()
BANKS = []
_b = 0
for _n in SIZES:
    _k = -(-_n * 16 // 512)
    BANKS.append([(_b + _i) % 8 for _i in range(_k)])
    _b += _k
CB = 7

SEMAPHORES = ["vec", "act", "ten", "gps", "loc", "gap"]
for _t in range(ST):
    SEMAPHORES += ["a%d_%d" % (_t, _j) for _j in range(NC)] + ["b%d" % _t]
SEMAPHORES += ["ld%d" % _k for _k in range(len(CP) + len(LP) + 2)] + ["st%d" % _k for _k in range(NC + 1)]

COST = {"cy": 0.83e-3, "gather": 1.4, "scatter": 3.0, "fix": 0.03, "gfix": 0.07, "lat": 0.05, "net": 2.0, "send": 0.9,
        "mm": 0.046, "ld0": 2.0, "ld": 1.4, "tab": 1.5}
NUDGE = {}
for _w in ("scan2_2:-6 min1_0:-1 lnS2:-5 diff1_1:7 scan3_3:5 lnS0:5 diff2_0:-5 min3_0:-2 scan3_1:-4 s2_0:2 gapc:6 vote2:8 min2_1:-7 G1_2:-6 min1_1:8 "
           "count:7 n3:2 n4:-2 scan2_3:-2 G2_1:-7 n1:6 decS0:1 s1_0:2 Iu0:-5 scan3_0:-3 Tr:-6").split():
    NUDGE[_w.split(":")[0]] = float(_w.split(":")[1])


def dur(ck, c):
    k, n = ck
    if k == "v":
        return c["fix"] + max(64, n) * c["cy"]
    if k == "s":
        return c["gfix"] + max(32, n) * c["cy"]
    if k == "stab":
        return c["tab"] + c["gfix"] + n * c["cy"]
    if k == "gather":
        return c["gfix"] + n * c["gather"] * c["cy"]
    if k == "scatter":
        return c["gfix"] + n * c["scatter"] * c["cy"]
    if k == "mm":
        return n * c["mm"]
    if k == "sel":
        return 0.2 + 2 * n * c["cy"]
    if k == "ld":
        return c["ld0"] + n * c["ld"]
    if k == "us":
        return n
    return n * c[k]


def plan(ops, c=COST, nudge=NUDGE):
    n = len(ops)
    cost = [dur(o["ck"], c) for o in ops]
    lat = c["lat"]
    succ = [[] for _ in range(n)]
    for i, o in enumerate(ops):
        for d in o["deps"]:
            succ[d].append(i)
    prio = [0.0] * n
    for i in range(n - 1, -1, -1):
        best = 0.0
        for k in succ[i]:
            best = max(best, prio[k] + lat)
        prio[i] = cost[i] + best
    prio = [p + nudge.get(o["name"], 0.0) for p, o in zip(prio, ops)]
    left = [len(o["deps"]) for o in ops]
    est = [0.0] * n
    ready = [i for i in range(n) if left[i] == 0]
    fin = [0.0] * n
    free = {}
    order = []
    beg = [0.0] * n
    while ready:
        pick, key = None, None
        for i in ready:
            q = ops[i]["q"]
            s = est[i] if q == "X" else max(est[i], free.get(q, 0.0))
            if key is None or (s, -prio[i]) < key:
                pick, key = i, (s, -prio[i])
        q = ops[pick]["q"]
        ready.remove(pick)
        order.append(pick)
        beg[pick] = key[0]
        fin[pick] = key[0] + cost[pick]
        if q != "X":
            free[q] = fin[pick]
        for k in succ[pick]:
            left[k] -= 1
            est[k] = max(est[k], fin[pick] + lat)
            if left[k] == 0:
                ready.append(k)
    return order, beg, fin


def build(g, T, topo, core, rank):
    A, F = AluOpType, ActivationFunctionType
    ops = []
    hist = {}

    def op(q, ck, fn, reads=(), writes=(), sem=None, deps=(), kind="c", name=""):
        i = len(ops)
        dd = set(deps)
        for lst, wr in ((reads, False), (writes, True)):
            for (b, lo, hi) in lst:
                for (l2, h2, k, w2) in hist.get(b, ()):
                    if k != i and l2 < hi and lo < h2 and (wr or w2):
                        dd.add(k)
        for (b, lo, hi) in writes:
            h = hist.get(b, [])
            hist[b] = [e for e in h if not (lo <= e[0] and e[1] <= hi)] + [(lo, hi, i, True)]
        for (b, lo, hi) in reads:
            hist.setdefault(b, []).append((lo, hi, i, False))
        ops.append({"q": q, "ck": ck, "fn": fn, "deps": dd, "sem": sem, "kind": kind, "name": name})
        return i

    def V(n, fn, reads, writes, name=""):
        return op("V", ("v", n), fn, reads, writes, name=name)

    def S(n, fn, reads, writes, name="", deps=(), k="s"):
        return op("S", (k, n), fn, reads, writes, name=name, deps=deps)

    def SG(n, fn, reads, writes, name=""):
        return op("S", ("gather", n), fn, reads, writes, name=name)

    def full(b):
        return (b, 0, 1 << 20)

    v, sc, te, sy = g.vector, g.scalar, g.tensor, g.sync

    for b, c in (("fK", KE), ("fN", -KE), ("fP", KV), ("fQ", -KV), ("fE", 1.0), ("hP", -3.5 * KV), ("hQ", 3.5 * KV), ("f1", 1.0), ("fF", 1.0), ("mask", 1.0)):
        V(512 if b == "mask" else 64, lambda b=b, c=c: v.memset(T[b][:], c), [], [full(b)], "fill")
    V(64, lambda: v.memset(T.mask[:, 0::16], 0.0), [], [full("mask")], "mask")
    for t in range(ST):
        V(64, lambda t=t: v.memset(T["MS%d" % t][:, CW:CT], 0.0), [], [("MS%d" % t, CW, CT)], "MSpad")

    def sel(out, src, n, pattern, cmp, base, cm):
        op("G", ("sel", n), lambda: g.affine_select(T[out][:], T[src][:], pattern, cmp, 0.0, base, cm), [full(src)], [full(out)], name="sel")

    op("G", ("us", 0.2), lambda: g.iota(T.pt[:], [[0, NQ]], 0, 1), [], [full("pt")], name="iota")
    op("G", ("us", 0.2), lambda: g.iota(T.q16[:], [[16, NQ]], 0, 0), [], [full("q16")], name="iota")
    for o, f in (("idN", "fN"), ("idK", "fK"), ("idF", "fF"), ("id1", "f1")):
        sel(o, f, 128, [[-1, 128]], A.is_equal, 0, 1)
    for x in "PQ":
        sel("b" + x + "1", "f" + x, 128, [[-16, 8], [0, 16]], A.is_ge, 0, 1)
        sel("b" + x, "b" + x + "1", 128, [[16, 8], [0, 16]], A.is_ge, 15, -1)
    sel("e1", "fE", 144, [[0, 9], [1, 16]], A.is_equal, -15, 0)
    sel("e2", "e1", 144, [[-16, 9], [0, 16]], A.is_ge, 0, 1)
    sel("e3", "e2", 144, [[16, 9], [0, 16]], A.is_ge, 15, -1)

    V(NQ, lambda: v.tensor_scalar(T.pa[:], T.pt[:], 15, None, A.bitwise_and), [full("pt")], [full("pa")])
    V(NQ, lambda: v.tensor_tensor(T.cl[:], T.pa[:], T.q16[:], A.add), [full("pa"), full("q16")], [full("cl")])
    V(NQ, lambda: v.tensor_scalar(T.c16[:], T.cl[:], 16.0, None, A.mult), [full("cl")], [full("c16")])
    for t in range(ST - 1):
        b = "TW%d" % t
        V(NQ, lambda b=b: v.tensor_scalar(T[b][:, 18:32], T.cl[:], 1.0, None, A.mult), [full("cl")], [(b, 18, 32)])

    dq = {"Y": sy, "S": sc}
    nld = [0]
    amount = [0]

    def load(q, out, in_, b, lo, hi):
        k = nld[0]
        nld[0] += 1
        amount[0] += hi - lo
        i = op(q, ("us", 0.06), lambda: dq[q].dma_start(out, in_), [], [], sem="ld%d" % k, kind="dma", name="ld")
        op("X", ("ld", amount[0] / 896.0), None, [], [(b, lo, hi)], sem=("ld%d" % k, 16), kind="arr", deps=[i], name="land")

    def load_c(q, p):
        lo, hi = CP[p]
        load(q, T.ck32[:, lo:hi], T.ck[:, lo:hi], "ck32", lo, hi)

    def load_l(q, p):
        lo, hi = LP[p]
        load(q, T.la32[:, lo:hi], T.la[:, lo:hi], "la32", lo, hi)

    load("Y", T.cu32[:], T.cu[:], "cu32", 0, NQ)
    load_c("Y", 0)
    load_l("S", 0)
    load_l("Y", 1)
    load_l("S", 2)
    load_l("Y", 3)
    load_c("S", 1)
    load("Y", T.gap32[:], T.gap[:], "gap32", 0, M)
    load_c("S", 2)
    load_c("Y", 3)

    V(NQ, lambda: v.tensor_copy(T.TW0[:, CW:CW + NQ], T.cu32[:]), [full("cu32")], [("TW0", CW, CW + NQ)])
    V(NQ, lambda: v.tensor_tensor(T.il32[:], T.cu32[:], T.c16[:], A.add), [full("cu32"), full("c16")], [full("il32")])
    V(NQ, lambda: v.tensor_copy(T.il[:], T.il32[:]), [full("il32")], [full("il")])
    for a, e in CHUNKS:
        op("V", ("gather", e - a), lambda a=a, e=e: v.tensor_copy(T.Iu[:, a:e], T.ck32[:, 0:16 * e].indirect(T.il[:, a // 16:e // 16])),
           [("ck32", 0, 16 * e), full("il")], [("Iu", a, e)], name="Iu0")
    exps = []

    def encode(src, f, o, lo, hi, q, k="s"):
        if q == "V":
            V(hi - lo, lambda: v.tensor_copy(T[f][:, lo:hi], T[src][:, lo:hi]), [(src, lo, hi)], [(f, lo, hi)], "conv")
        else:
            op("G", ("sel", hi - lo), lambda: g.affine_select(T[f][:, lo:hi], T[src][:, lo:hi], [[0, hi - lo]], A.is_ge, 0.0, 0, 0), [(src, lo, hi)], [(f, lo, hi)], name="convg")
        exps.append(S(hi - lo, lambda: sc.activation(T[o][:, lo:hi], T[f][:, lo:hi], F.Exp, bias=B0, scale=1.0 / SC), [(f, lo, hi)], [(o, lo, hi)], name="exp", k=k))

    encode("ck32", "cf", "Cc", CP[0][0], CP[0][1], "V", "stab")
    for lo, hi in LP:
        encode("la32", "lf", "Lc", lo, hi, "V")
    for lo, hi in CP[1:]:
        encode("ck32", "cf", "Cc", lo, hi, "G")
    V(M, lambda: v.tensor_scalar(T.gapf[:], T.gap32[:], 0.5, None, A.subtract), [full("gap32")], [full("gapf")])
    exps.append(S(M, lambda: sc.activation(T.gc0[:], T.gapf[:], F.Exp, scale=1.0 / SC), [full("gapf")], [full("gc0")], name="expg"))

    nloc = [0]
    cores = list(T.cores)
    nxt = cores[(rank + 1) % len(cores)]

    def send_gap():
        dst = [cores[(rank + d) % len(cores)] for d in (1, 2)]
        eng = [e for e in topo.engines(core, dst[0]) if e in topo.engines(core, dst[1])]
        m = 0
        for e in eng:
            m |= 1 << e
        ids = []
        for d in dst:
            a = topo.addr(d)
            ids.append(DstId(rid=a[0], pnc=a[1]))
        nloc[0] += len(eng)
        g.remote_dma_fused([RemoteDMATransfer(dst_ids=ids, dma_engine_mask=m, remote_sem=T.sem.gap, srcs=[T.gc0[:]], dsts=[T.gc1[:], T.gc2[:]])], local_sem=T.sem.loc)

    i = op("G", ("send", 1), send_gap, [full("gc0")], [], kind="send", name="gap")
    ne = len(topo.engines(core, nxt))
    op("X", ("us", 5.0), None, [], [full("gc1"), full("gc2")], sem=("gap", 2 * ne), kind="arr", deps=[i], name="agap")

    def send(out, in_, sem):
        a = topo.addr(nxt)
        nloc[0] += ne
        g.remote_dma(out, in_, T.sem[sem], T.sem.loc, a[1], a[0], topo.mask(core, nxt))

    cn = "ps%d" % CB
    pc = T[cn]
    SG(M, lambda: sc.activation(T.Ic0[:], T.Cc[:, 0:W].indirect(T.il[:]), F.Copy), [("Cc", 0, W), full("il")], [full("Ic0")], name="Ic0")

    def step(t):
        last = t == ST - 1
        IC, TW, MS, IP = "Ic%d" % t, "TW%d" % t, "MS%d" % t, "IP%d" % t
        Icb, TWb, MSb, IPb = T[IC], T[TW], T[MS], T[IP]
        if not last:
            gb = "gc%d" % t
            op("P", ("mm", 14), lambda: te.matmul(pc[:, 16:240], T.idF[:], T[gb][:], True, True), [full("idF"), full(gb)], [full(cn)], name="gapc")
            if t == 0:
                V(M, lambda: v.tensor_tensor(TWb[:, CT:CR], T.Ic0[:], pc[:, 16:240], A.mult), [full("Ic0"), full(cn)], [("TW0", CT, CR)], "Tc0")
        for j, (a, e) in enumerate(CHUNKS):
            n = e - a
            xb, yb, Pb, ub = T["x%d" % j], T["y%d" % j], T["P%d" % j], T["u%d" % j]
            X, Y, P, U = "x%d" % j, "y%d" % j, "P%d" % j, "u%d" % j
            if t > 0:
                S(n, lambda a=a, e=e: sc.activation(T.lnI[:, a:e], Icb[:, a:e], F.Ln, scale=UP), [(IC, a, e)], [("lnI", a, e)], name="lnI%d" % j)
                V(n, lambda a=a, e=e: v.tensor_scalar(T.Iu[:, a:e], T.lnI[:, a:e], SC, OFF + 0.25, A.mult, A.add), [("lnI", a, e)], [("Iu", a, e)], "decI%d" % j)
            SG(16 * n, lambda a=a, e=e, xb=xb: sc.activation(xb[:], T.Lc[:].indirect(T.Iu[:, a:e]), F.Copy), [full("Lc"), ("Iu", a, e)], [full(X)], name="G1_%d" % j)
            V(8 * n, lambda n=n, xb=xb, Pb=Pb: v.tensor_tensor_scan(Pb[:], T.mask[:, 0:16 * n], xb[:], 0.0, A.mult, A.max), [full("mask"), full(X)], [full(P)], "scan1_%d" % j)
            bk = BANKS[j]
            per = 16 // len(bk)
            for h, b in enumerate(bk):
                def diff(n=n, xb=xb, Pb=Pb, h=h, k=len(bk), per=per, pb=T["ps%d" % b]):
                    te.matmul(pb[:, 0:per * n], T.idN[:], xb[:, h::k], True, False)
                    for i in range(per):
                        r = te.matmul(pb[:, i:per * n:per], T.idK[:], Pb[:, 15::16], False, i == per - 1)
                    return r

                op("P", ("mm", per + per * n / 64), diff, [full("idK"), full("idN"), full(P), full(X)], [full("ps%d" % b)], name="diff%d_%d" % (j, h))
                V(per * n, lambda n=n, xb=xb, yb=yb, h=h, k=len(bk), per=per, pb=T["ps%d" % b]: v.tensor_tensor(yb[:, h::k], xb[:, h::k], pb[:, 0:per * n], A.min),
                  [full(X), full("ps%d" % b)], [(Y, h, h + 1)], "min%d_%d" % (j, h))
            V(8 * n, lambda n=n, yb=yb, ub=ub: v.tensor_tensor_scan(ub[:], T.mask[:, 0:16 * n], yb[:], 0.0, A.mult, A.max), [full("mask"), full(Y)], [full(U)], "scan2_%d" % j)
            S(n, lambda a=a, e=e, ub=ub: sc.activation(T.lnS[:, a:e], ub[:, 15::16], F.Ln, bias=EPS, scale=UP), [full(U)], [("lnS", a, e)],
              deps=exps if t == 0 else (), name="lnS%d" % j, k="stab" if t == 0 and j == 0 else "s")
            V(n, lambda a=a, e=e: v.tensor_scalar(T.su[:, a:e], T.lnS[:, a:e], SC, OFF + 0.25, A.mult, A.add), [("lnS", a, e)], [("su", a, e)], "decS%d" % j)
        V(NQ, lambda: v.tensor_copy(T.ni[:, 0:14], TWb[:, CW:CW + NQ]), [(TW, CW, CW + NQ)], [("ni", 0, 14)], "n0")
        V(NQ, lambda: v.tensor_scalar(T.ni[:, 14:28], TWb[:, CW:CW + NQ], 1.0, None, A.add), [(TW, CW, CW + NQ)], [("ni", 14, 28)], "n1")
        V(NQ, lambda: v.tensor_scalar(T.nw[:], T.ni[:], 15, None, A.bitwise_and), [full("ni")], [full("nw")], "n2")
        V(NQ, lambda: v.tensor_tensor(T.rl32[:], T.nw[:, 14:28], T.c16[:], A.add), [full("nw"), full("c16")], [full("rl32")], "n3")
        V(NQ, lambda: v.tensor_copy(T.rl[:], T.rl32[:]), [full("rl32")], [full("rl")], "n4")
        if not last:
            V(NQ, lambda: v.tensor_tensor(TWb[:, 4:18], T.nw[:, 0:14], T.c16[:], A.add), [full("nw"), full("c16")], [(TW, 4, 18)], "n5")
        SG(M, lambda: sc.activation(T.Rld[:], T.Cc[:, 0:W].indirect(T.rl[:]), F.Copy), [("Cc", 0, W), full("rl")], [full("Rld")], name="Rld")
        if not last:
            V(M, lambda: v.tensor_tensor(TWb[:, CR:CE], T.Rld[:], pc[:, 16:240], A.mult), [full("Rld"), full(cn)], [(TW, CR, CE)], "Tr")
        for j, (a, e) in enumerate(CHUNKS):
            n = e - a
            zb, qb = T["z%d" % j], T["q%d" % j]
            Z, Q = "z%d" % j, "q%d" % j
            pn, qn = "ps%d" % BANKS[j][0], "ps%d" % BANKS[j][-1]
            pb, qp = T[pn], T[qn]

            def prep(a=a, e=e, n=n, qp=qp):
                te.matmul(qp[:, 256:256 + n], T.id1[:], Icb[:, a:e], True, True)
                return te.matmul(qp[:, 320:320 + n], T.idF[:], TWb[:, CT + a:CT + e], True, True)

            op("P", ("mm", 5), prep, [full("id1"), full("idF"), (IC, a, e), (TW, CT + a, CT + e)], [full(qn)], name="prep%d" % j)
            SG(16 * n, lambda a=a, e=e, zb=zb: sc.activation(zb[:], T.Cc[:, 0:W].indirect(T.su[:, a:e]), F.Copy), [("Cc", 0, W), ("su", a, e)], [full(Z)], name="G2_%d" % j)
            V(8 * n, lambda n=n, zb=zb, qb=qb: v.tensor_tensor_scan(qb[:], T.mask[:, 0:16 * n], zb[:], 0.0, A.mult, A.max), [full("mask"), full(Z)], [full(Q)], "scan3_%d" % j)
            V(n, lambda a=a, e=e, n=n, qb=qb, qp=qp: v.tensor_tensor(T.Inew[:, a:e], qb[:, 15::16], qp[:, 256:256 + n], A.max), [full(qn), full(Q)], [("Inew", a, e)], "Inew%d" % j)
            V(n, lambda a=a, e=e, n=n, qp=qp: v.tensor_tensor(T.R[:, a:e], T.Inew[:, a:e], qp[:, 320:320 + n], A.is_ge), [("Inew", a, e), full(qn)], [("R", a, e)], "R%d" % j)

            def votes(a=a, e=e, n=n, pb=pb):
                for k, (w, h) in enumerate((("bP", "hP"), ("bQ", "hQ"))):
                    o = pb[:, k * n:k * n + n]
                    te.matmul(o, T[w][:], T.R[:, a:e], True, False)
                    r = te.matmul(o, T[h][0:1, :], T.f1[0:1, 0:n], False, True)
                return r

            op("P", ("mm", 4), votes, [full("bP"), full("bQ"), full("hP"), full("hQ"), full("f1"), ("R", a, e)], [full(pn)], name="vote%d" % j)
            V(n, lambda a=a, e=e, n=n, pb=pb: v.tensor_tensor(T.s2[:, a:e], T.Inew[:, a:e], pb[:, n:2 * n], A.min), [("Inew", a, e), full(pn)], [("s2", a, e)], "s2_%d" % j)
            V(n, lambda a=a, e=e, n=n, pb=pb: v.tensor_tensor(pb[:, 128:128 + n], T.Rld[:, a:e], pb[:, 0:n], A.min), [("Rld", a, e), full(pn)], [full(pn)], "s1_%d" % j)
            V(n, lambda a=a, e=e, n=n, pb=pb: v.tensor_tensor(IPb[:, a:e], T.s2[:, a:e], pb[:, 128:128 + n], A.max), [full(pn), ("s2", a, e)], [(IP, a, e)], "IP%d" % j)
            nm = "a%d_%d" % (t, j)
            i = op("G", ("send", 1), lambda a=a, e=e, nm=nm: send(T["Ic%d" % (t + 1)][:, a:e], IPb[:, a:e], nm), [(IP, a, e)], [], kind="send", name="A%d" % j)
            op("X", ("net", 1), None, [], [("Ic%d" % (t + 1), a, e)], sem=(nm, ne), kind="arr", deps=[i], name="arrA%d" % j)

        def count():
            for p in range(16):
                r = te.matmul(pc[:, 0:NQ], T.e3[:, 15 - p:143 - p], T.R[:, p::16], p == 0, p == 15)
            return r

        op("P", ("mm", 16), count, [full("e3"), full("R")], [full(cn)], name="count")
        lo = 28 if last else 0
        if not last:
            V(NQ, lambda: v.tensor_scalar(T.pm[:, 0:14], pc[:, 0:NQ], 3.5, float(W), A.is_lt, A.mult), [full(cn)], [("pm", 0, 14)], "c0")
            V(NQ, lambda: v.tensor_scalar(T.pm[:, 14:28], pc[:, 0:NQ], 3.5, float(M), A.is_ge, A.mult), [full(cn)], [("pm", 14, 28)], "c1")
        V(NQ, lambda: v.tensor_scalar(T.pm[:, 28:42], pc[:, 0:NQ], 3.5, None, A.is_ge), [full(cn)], [("pm", 28, 42)], "c2")
        V(42, lambda: v.tensor_tensor(MSb[:, 4 + lo:46], T.pm[:, lo:42], TWb[:, 4 + lo:46], A.add), [("pm", lo, 42), (TW, 4 + lo, 46)], [(MS, 4 + lo, 46)], "c3")
        if not last:
            V(28, lambda: v.tensor_copy(T.lst[:], MSb[:, 4:32]), [(MS, 4, 32)], [full("lst")], "c4")
            SG(M, lambda: sc.activation(MSb[:, CT:CR], TWb[:, CT:CE].indirect(T.lst[:, 14:28]), F.Copy), [(TW, CT, CE), full("lst")], [(MS, CT, CR)], name="Tsel")
            op("V", ("scatter", M), lambda: v.tensor_copy(T.Cc[:].indirect(T.lst[:, 0:14]), T.Inew[:]), [full("Inew"), full("lst")], [full("Cc")], name="scatter")
        hi = CT if last else CR
        i = op("G", ("send", 1), lambda: send(T["TW%d" % (t + 1)][:, CW:hi], MSb[:, CW:hi], "b%d" % t), [(MS, CW, hi)], [], kind="send", name="B")
        op("X", ("net", 1), None, [], [("TW%d" % (t + 1), CW, hi)], sem=("b%d" % t, ne), kind="arr", deps=[i], name="arrB")

    for t in range(ST):
        step(t)
    IC, TW = "Ic%d" % ST, "TW%d" % ST
    Fb, Lb = T[IC], T[TW]
    for j, (a, e) in enumerate(CHUNKS):
        n = e - a
        S(n, lambda a=a, e=e: sc.activation(T.lnI[:, a:e], Fb[:, a:e], F.Ln, scale=UP), [(IC, a, e)], [("lnI", a, e)], name="lnY")
        V(n, lambda a=a, e=e: v.tensor_scalar(T.yint[:, a:e], T.lnI[:, a:e], SC, OFF, A.mult, A.add), [("lnI", a, e)], [("yint", a, e)])
        V(n, lambda a=a, e=e: v.tensor_copy(T.yout[:, a:e], T.yint[:, a:e]), [("yint", a, e)], [("yout", a, e)])
        op("Y", ("us", 0.1), lambda a=a, e=e: sy.dma_start(T.yi[:, a:e], T.yout[:, a:e]), [("yout", a, e)], [], sem="st%d" % j, kind="dma", name="yi")
    V(NQ, lambda: v.tensor_copy(T.ni[:, 0:14], Lb[:, CW:CW + NQ]), [(TW, CW, CW + NQ)], [("ni", 0, 14)])
    V(NQ, lambda: v.tensor_scalar(T.nw[:, 0:14], T.ni[:, 0:14], 15, None, A.bitwise_and), [("ni", 0, 14)], [("nw", 0, 14)])
    V(NQ, lambda: v.tensor_copy(Lb[:, 4:18], T.nw[:, 0:14]), [("nw", 0, 14)], [(TW, 4, 18)])
    op("Y", ("us", 0.1), lambda: sy.dma_start(T.yc[:], Lb[:, 4:18]), [(TW, 4, 18)], [], sem="st%d" % NC, kind="dma", name="yc")
    return ops, nloc


SEMOF = {"V": "vec", "S": "act", "P": "ten", "G": "gps"}


def emit(g, T, ops, order):
    eng = {"V": g.vector, "S": g.scalar, "P": g.tensor, "G": g, "Y": g.sync}
    cnt = {"vec": 0, "act": 0, "ten": 0, "gps": 0}
    seen = {q: {} for q in eng}
    tok = {}
    for i in order:
        o = ops[i]
        if o["q"] == "X":
            tok[i] = (o["sem"][0], o["sem"][1], {o["sem"][0]: o["sem"][1]})
            continue
        q = o["q"]
        s = seen[q]
        toks = sorted([tok[d] for d in o["deps"] if tok.get(d) is not None], key=lambda x: (-sum(x[2].values()), x[0]))
        top = {}
        for sem, val, clock in toks:
            top[sem] = max(top.get(sem, 0), val)
        for sem, val, clock in toks:
            if s.get(sem, 0) >= val or top[sem] > val:
                continue
            eng[q].wait_ge(T.sem[sem], val)
            for k, w in clock.items():
                s[k] = max(s.get(k, 0), w)
        r = o["fn"]()
        tok[i] = None
        if o["kind"] == "c":
            sem = SEMOF[q]
            cnt[sem] += 1
            r.then_inc(T.sem[sem], 1)
            c = dict(s)
            c[sem] = cnt[sem]
            tok[i] = (sem, cnt[sem], c)
        elif o["kind"] == "dma":
            r.then_inc(T.sem[o["sem"]], 16)
    for sem in sorted(cnt):
        g.wait_ge(T.sem[sem], cnt[sem])


def rank_program(g, core, T, topo):
    rank = T.rank_of(core)
    if rank is None:
        return
    ops, nloc = build(g, T, topo, core, rank)
    order, beg, fin = plan(ops)
    emit(g, T, ops, order)
    for k in range(NC + 1):
        g.wait_ge(T.sem["st%d" % k], 16)
    g.wait_ge(T.sem.loc, nloc[0])
